import numpy as np
import ml_dtypes


def mxq(x, axis, fmt="e4m3"):
    dtype, down = {"e4m3": (ml_dtypes.float8_e4m3fn, 7), "e5m2": (ml_dtypes.float8_e5m2, 14)}[fmt]
    v = np.moveaxis(np.asarray(x, np.float32).astype(ml_dtypes.bfloat16).astype(np.float64), axis, -1)
    blocks = v.reshape(v.shape[:-1] + (-1, 32))
    amax = np.abs(blocks).max(-1, keepdims=True)
    byte = np.maximum(np.where(amax > 0, np.frexp(amax)[1] - 1 + 127, 0) - down, 1)
    scale = np.exp2(byte - 127.0)
    codes = (blocks / scale).astype(np.float32).astype(dtype).astype(np.float64)
    return np.moveaxis((codes * scale).reshape(v.shape), -1, axis)


WIDE = False


def mx_kscale(k):
    if not WIDE:
        return np.ones(k)
    levels = np.array([10, -10, 5, -5, 0])
    if k % 512:
        return np.exp2(np.random.permutation(np.resize(levels, k // 32))).repeat(32)
    a = np.empty((k // 512, 16))
    for p in range(k // 512):
        a[p, :8] = np.random.permutation(np.resize(levels, 8))
        for g in range(8):
            far = levels[np.abs(levels - a[p, g]) >= 10]
            a[p, g + 8] = far[np.random.randint(len(far))]
    return np.exp2(a.ravel()).repeat(32)


def f64(x):
    return np.asarray(x).astype(np.float64)


E2M1 = np.array([0.0, 0.5, 1.0, 1.5, 2.0, 3.0, 4.0, 6.0, -0.0, -0.5, -1.0, -1.5, -2.0, -3.0, -4.0, -6.0])


def pack_weight(w, fmt):
    k, n = w.shape
    w = f64(np.asarray(w, np.float32).astype(ml_dtypes.bfloat16)).reshape(k // 32, 32, n)
    amax = np.abs(w).max(1)
    if fmt == "e4m3":
        byte = np.frexp(amax)[1] - 1 + 127 - 7
    else:
        mant, ex = np.frexp(amax / 6.0)
        byte = np.where(mant > 0.5, ex, ex - 1) + 127
    byte = np.clip(np.where(amax > 0, byte, 1), 1, 254)
    scaled = (w * np.exp2(127.0 - byte)[:, None, :]).reshape(k, n).astype(np.float32)
    by_word = np.ascontiguousarray(scaled.reshape(k // 512, 128, 4, n).transpose(0, 1, 3, 2))
    if fmt == "e4m3":
        words = by_word.astype(ml_dtypes.float8_e4m3fn).view(np.uint8)
    else:
        c = by_word.astype(ml_dtypes.float4_e2m1fn).view(np.uint8) & 0xF
        words = (c[..., 0::2] | (c[..., 1::2] << 4)).reshape(k // 512, 128, 2 * n)
    return np.ascontiguousarray(words), np.ascontiguousarray(byte.astype(np.uint8).reshape(k // 512, 16, n))


def unpack_weight(words, scales, fmt):
    g, _, n = scales.shape
    words = np.ascontiguousarray(words).reshape(g, 128, n, -1)
    if fmt == "e4m3":
        vals = words.view(ml_dtypes.float8_e4m3fn).astype(np.float64)
    else:
        nib = np.empty((g, 128, n, 4), np.uint8)
        nib[..., 0::2] = words & 0xF
        nib[..., 1::2] = words >> 4
        vals = E2M1[nib]
    vals = vals * np.repeat(np.exp2(scales.astype(np.float64) - 127.0), 8, axis=1)[..., None]
    return vals.transpose(0, 1, 3, 2).reshape(g * 512, n)


def bf(x):
    return np.asarray(x, np.float32).astype(ml_dtypes.bfloat16)


def planes(Y):
    r, m = Y.shape
    b = f64(bf(Y)).reshape(r // 32, 32, m)
    amax = np.abs(b).max(1)
    byte = np.clip(np.where(amax > 0, np.frexp(amax)[1] - 1 + 127 - 7, 1), 1, 254)
    codes = (b * np.exp2(127.0 - byte)[:, None, :]).reshape(r, m).astype(np.float32).astype(ml_dtypes.float8_e4m3fn).view(np.uint8)
    words = codes.reshape(r // 512, 128, 4, m).transpose(0, 1, 3, 2)
    return np.ascontiguousarray(words), np.ascontiguousarray(byte.astype(np.uint8).reshape(r // 512, 16, m))


K, L, T, R, N, B = 512, 512, 1024, 512, 512, 512


def setup_inputs():
    n = np.random.standard_normal
    fk = mx_kscale(K)
    fr = mx_kscale(R)
    fl = mx_kscale(L)
    xtp = pack_weight(n((K, T)) / fk[:, None], "e2m1")
    wap = pack_weight(n((K, R)) * 1 / np.sqrt(K) * fk[:, None] * fr, "e4m3")
    xqp = pack_weight(n((L, T)) / fl[:, None], "e2m1")
    wcp = pack_weight(n((L, R)) * 1 / np.sqrt(L) * fl[:, None] * fr, "e4m3")
    wbp = pack_weight(n((R, N)) * 1 / np.sqrt(R) / fr[:, None], "e2m1")
    wyp = pack_weight(n((K, N)) * 1 / np.sqrt(K) * fk[:, None], "e4m3")
    return {
        "xt_words": xtp[0],
        "xt_scales": xtp[1],
        "wa_words": wap[0],
        "wa_scales": wap[1],
        "xq_words": xqp[0],
        "xq_scales": xqp[1],
        "wc_words": wcp[0],
        "wc_scales": wcp[1],
        "wb_words": wbp[0],
        "wb_scales": wbp[1],
        "wy_words": wyp[0],
        "wy_scales": wyp[1],
    }


def reference(xt_words, xt_scales, wa_words, wa_scales, xq_words, xq_scales, wc_words, wc_scales, wb_words, wb_scales, wy_words, wy_scales):
    xtu = unpack_weight(xt_words, xt_scales, "e2m1")
    wau = unpack_weight(wa_words, wa_scales, "e4m3")
    xqu = unpack_weight(xq_words, xq_scales, "e2m1")
    wcu = unpack_weight(wc_words, wc_scales, "e4m3")
    wbu = unpack_weight(wb_words, wb_scales, "e2m1")
    wyu = unpack_weight(wy_words, wy_scales, "e4m3")
    z = wau.T @ xtu + wcu.T @ xqu
    hid = z.reshape(R, B, T // B).max(axis=2)
    hidq = mxq(hid, 0, "e4m3")
    p = wbu.T @ hidq
    pr = np.repeat(p, T // B, axis=1)
    q = wyu.T @ xtu
    y = np.tanh(pr) + q
    words, scales = planes(y)
    return y, words, scales

@@ -1,0 +1,290 @@
+from contextlib import ExitStack
+
+import concourse.mybir as mybir
+
+K, T, R, N, B = 512, 1024, 512, 512, 512
+FLOPS = 2 * K * R * T * 2 + 2 * K * N * T + 2 * R * N * B
+
+F32 = mybir.dt.float32
+BF16 = mybir.dt.bfloat16
+I32 = mybir.dt.int32
+U8 = mybir.dt.uint8
+FP8X4 = mybir.dt.float8_e4m3fn_x4
+FP4X4 = mybir.dt.float4_e2m1fn_x4
+ALU = mybir.AluOpType
+ACT = mybir.ActivationFunctionType
+
+P = 128
+WA, WC, WY, WB = 0, 1, 2, 3
+XT, XQ = 0, 1
+
+
+def tile_mix_hidden_peaks_of_pairs_pl_kernel(
+    tc, xt_words, xt_scales, wa_words, wa_scales, xq_words, xq_scales, wc_words, wc_scales,
+    wb_words, wb_scales, wy_words, wy_scales, out_0, out_1, out_2,
+):
+    nc = tc.nc
+    with ExitStack() as ctx:
+        sb = ctx.enter_context(tc.tile_pool(name="sb", bufs=1))
+        ps = ctx.enter_context(tc.psum_pool(name="ps", bufs=1))
+        ctx.enter_context(tc.manual_schedule())
+
+        def sbuf(name, width, dtype):
+            return sb.tile([P, width], dtype, name=name, align_bytes=256)
+
+        raw_sc = sbuf("raw_sc", 512, U8)
+        stage = sbuf("stage", 1024, U8)
+        plane = sbuf("plane", 4096, U8)
+        raw_w = [sbuf("raw_w%d" % w, 512, I32) for w in (WA, WC, WY)]
+        raw_wb = sbuf("raw_wb", 1024, U8)
+        dealt = [sbuf("dealt%d" % w, 512, I32) for w in (WA, WC, WY)]
+        dealt_wb = sbuf("dealt_wb", 1024, U8)
+        x = [sbuf("x%d" % s, 2048, U8) for s in (XT, XQ)]
+        odd_sb = [sbuf("odd%d" % u, 256, F32) for u in range(8)]
+        hid = [sbuf("hid%d" % c, 512, BF16) for c in range(4)]
+        hq = [sbuf("hq%d" % c, 128, I32) for c in range(4)]
+        hs = [sbuf("hs%d" % c, 128, U8) for c in range(4)]
+        th_sb = [sbuf("th%d" % c, 512, F32) for c in range(4)]
+        y = [sbuf("y%d" % c, 1024, F32) for c in range(4)]
+        yb = [sbuf("yb%d" % c, 1024, BF16) for c in range(4)]
+        yq = sbuf("yq", 1024, I32)
+        ys = sbuf("ys", 1024, U8)
+        zb = [ps.tile([P, 512], F32, name="zb%d" % i) for i in range(3)]
+        qb = [ps.tile([P, 512], F32, name="qb%d" % i) for i in range(4)]
+        pb = ps.tile([P, 512], F32, name="pb")
+
+        def w_scale(w, j):
+            return plane[:, 1024 * w + 128 * j : 1024 * w + 128 * (j + 1)]
+
+        def x_scale(s, t0, n):
+            c0 = 1024 * (2 * (t0 // 512) + s) + 512 + t0 % 512
+            return plane[:, c0 : c0 + n]
+
+        def x_codes(s, t0, n):
+            return x[s][:, 2 * t0 : 2 * (t0 + n)].bitcast(FP4X4)
+
+        def load_w_scales(eng, w, src):
+            eng.dma_start(out=raw_sc[:].bitcast(I32)[w:64:4, :], in_=src[0].bitcast(I32))
+
+        def load_x_scales(eng, s, src):
+            eng.dma_start(
+                out=stage[:].bitcast(I32)[s:64:2, 128:256],
+                in_=src[0].rearrange("q (h c) -> (q h) c", h=2).bitcast(I32),
+            )
+
+        def load_w(w, src):
+            nc.sync.dma_start(out=raw_w[w][:], in_=src[0].rearrange("p n t -> p (n t)").bitcast(I32))
+
+        def deal(w):
+            nc.vector.tensor_copy(
+                out=dealt[w][:].rearrange("p (j m) -> p m j", j=4),
+                in_=raw_w[w][:].rearrange("p (m j) -> p m j", j=4),
+            )
+
+        def deal_wb():
+            nc.vector.tensor_copy(
+                out=dealt_wb[:].rearrange("p (j m e) -> p j m e", j=4, e=2),
+                in_=raw_wb[:].rearrange("p (m j e) -> p j m e", j=4, e=2),
+            )
+
+        def z(u):
+            bank = zb[u % 3]
+            for j in range(4):
+                for w, s in ((WA, XT), (WC, XQ)):
+                    nc.tensor.matmul_mx(
+                        out=bank[:, 128 * j : 128 * (j + 1)],
+                        lhsT=dealt[w][:, 128 * j : 128 * (j + 1)].bitcast(FP8X4),
+                        lhsT_scale=w_scale(w, j),
+                        rhs=x_codes(s, 128 * u, 128),
+                        rhs_scale=x_scale(s, 128 * u, 128),
+                        start=(w == WA),
+                        stop=(w == WC),
+                    )
+
+        def pairs(u):
+            return zb[u % 3][:].rearrange("p (j b e) -> p b j e", j=4, e=2)
+
+        def hid_half(u):
+            return hid[u // 2][:, 256 * (u % 2) : 256 * (u % 2 + 1)].rearrange("p (b j) -> p b j", j=4)
+
+        def red(u):
+            nc.vector.tensor_reduce(out=hid_half(u), in_=pairs(u), axis=mybir.AxisListType.X, op=ALU.max)
+
+        def odd(u):
+            nc.scalar.copy(out=odd_sb[u][:].rearrange("p (b j) -> p b j", j=4), in_=pairs(u)[:, :, :, 1])
+
+        def mx(u):
+            nc.vector.tensor_tensor(
+                out=hid_half(u), in0=pairs(u)[:, :, :, 0],
+                in1=odd_sb[u][:].rearrange("p (b j) -> p b j", j=4), op=ALU.max,
+            )
+
+        def qh(c):
+            nc.vector.quantize_mx(out=hq[c][:].bitcast(FP8X4), scales=hs[c][:], in_=hid[c][:])
+
+        def p(c):
+            for i in range(4):
+                nc.tensor.matmul_mx(
+                    out=pb[:, 128 * i : 128 * (i + 1)],
+                    lhsT=dealt_wb[:, 256 * i : 256 * (i + 1)].bitcast(FP4X4),
+                    lhsT_scale=w_scale(WB, i),
+                    rhs=hq[c][:].bitcast(FP8X4),
+                    rhs_scale=hs[c][:],
+                    start=True,
+                    stop=True,
+                )
+
+        def th(c):
+            nc.scalar.activation(out=th_sb[c][:], in_=pb[:], func=ACT.Tanh)
+
+        def q(c):
+            for i in range(4):
+                bank = qb[2 * (c % 2) + i // 2]
+                nc.tensor.matmul_mx(
+                    out=bank[:, 256 * (i % 2) : 256 * (i % 2 + 1)],
+                    lhsT=dealt[WY][:, 128 * i : 128 * (i + 1)].bitcast(FP8X4),
+                    lhsT_scale=w_scale(WY, i),
+                    rhs=x_codes(XT, 256 * c, 256),
+                    rhs_scale=x_scale(XT, 256 * c, 256),
+                    start=True,
+                    stop=True,
+                )
+
+        rows = out_0.rearrange("(p i) t -> p i t", i=4)
+
+        def add(c, h):
+            part = y[c][:, 512 * h : 512 * (h + 1)]
+            nc.vector.tensor_tensor(
+                out=part.rearrange("p (b e) -> p b e", e=2),
+                in0=qb[2 * (c % 2) + h][:].rearrange("p (b e) -> p b e", e=2),
+                in1=th_sb[c][:, 256 * h : 256 * (h + 1)].unsqueeze(2).broadcast_to([P, 256, 2]),
+                op=ALU.add,
+            )
+            nc.sync.dma_start(
+                out=rows[:, 2 * h : 2 * h + 2, 256 * c : 256 * (c + 1)],
+                in_=part.rearrange("p (i t) -> p i t", i=2),
+            )
+
+        def cast_views(u):
+            c, h = divmod(u, 2)
+            src = y[c][:].rearrange("p (i h g e) -> p h g i e", i=4, h=2, e=4)[:, h]
+            dst = yb[c][:, 512 * h : 512 * (h + 1)].rearrange("p (g e i) -> p g i e", e=4, i=4)
+            return dst, src
+
+        def cS(u):
+            dst, src = cast_views(u)
+            nc.scalar.copy(out=dst, in_=src)
+
+        def cV(u):
+            dst, src = cast_views(u)
+            nc.vector.tensor_copy(out=dst, in_=src)
+
+        words = out_1[0].rearrange("p c r -> p (c r)").bitcast(I32)
+
+        def quant_y(c, t0, n):
+            cols = slice(256 * c + t0, 256 * c + t0 + n)
+            nc.vector.quantize_mx(out=yq[:, cols].bitcast(FP8X4), scales=ys[:, cols], in_=yb[c][:, 4 * t0 : 4 * (t0 + n)])
+
+        def st1(c):
+            nc.sync.dma_start(out=words[:, 256 * c : 256 * (c + 1)], in_=yq[:, 256 * c : 256 * (c + 1)])
+
+        def qY(c):
+            quant_y(c, 0, 256)
+            st1(c)
+
+        def qy(u):
+            quant_y(u // 2, 128 * (u % 2), 128)
+
+
+        nc.vector.memset(raw_sc[:].bitcast(I32)[64:128, :], 0)
+        nc.vector.memset(plane[:].bitcast(I32), 0)
+        load_w_scales(nc.sync, WA, wa_scales)
+        load_w_scales(nc.scalar, WY, wy_scales)
+        load_w_scales(nc.sync, WC, wc_scales)
+        load_w_scales(nc.scalar, WB, wb_scales)
+        load_x_scales(nc.sync, XT, xt_scales)
+        load_x_scales(nc.scalar, XQ, xq_scales)
+        load_w(WA, wa_words)
+        load_w(WC, wc_words)
+        nc.sync.dma_start(out=x[XT][:].bitcast(I32), in_=xt_words[0].bitcast(I32))
+        nc.sync.dma_start(out=x[XQ][:].bitcast(I32), in_=xq_words[0].bitcast(I32))
+        load_w(WY, wy_words)
+        nc.sync.dma_start(out=raw_wb[:].bitcast(I32), in_=wb_words[0].bitcast(I32))
+        nc.vector.tensor_copy(
+            out=stage[:, 0:512].rearrange("p (j m) -> p j m", j=4),
+            in_=raw_sc[:].rearrange("p (m j) -> p j m", j=4),
+        )
+        for quad in range(4):
+            nc.scalar.dma_start(
+                out=plane[:].bitcast(I32)[32 * quad : 32 * quad + 4, :],
+                in_=stage[:].bitcast(I32)[16 * quad : 16 * quad + 16, :],
+            )
+        deal(WA)
+        deal(WC)
+
+        deal(WY)
+        deal_wb()
+        z(0)
+        z(1)
+        red(0)
+        red(1)
+        z(2)
+        qh(0)
+        red(2)
+        z(3)
+        p(0)
+        th(0)
+        red(3)
+        q(0)
+        qh(1)
+        z(4)
+        odd(4)
+        add(0, 0)
+        z(5)
+        p(1)
+        mx(4)
+        odd(5)
+        add(0, 1)
+        th(1)
+        mx(5)
+        z(6)
+        q(1)
+        cS(0)
+        qh(2)
+        odd(6)
+        z(7)
+        p(2)
+        add(1, 0)
+        cS(1)
+        mx(6)
+        odd(7)
+        add(1, 1)
+        q(2)
+        mx(7)
+        th(2)
+        qY(0)
+        qh(3)
+        p(3)
+        q(3)
+        cS(2)
+        add(2, 0)
+        th(3)
+        add(2, 1)
+        cS(3)
+        add(3, 0)
+        cS(4)
+        qY(1)
+        add(3, 1)
+        cS(5)
+        cV(7)
+        cS(6)
+        qY(2)
+        qy(7)
+        qy(6)
+        st1(3)
+        for quad in range(4):
+            eng = nc.scalar if quad % 2 else nc.sync
+            eng.dma_start(
+                out=out_2[0, 4 * quad : 4 * quad + 4, :].bitcast(I32),
+                in_=ys[:].bitcast(I32)[32 * quad : 32 * quad + 4, :],
+            )

@@ -2,8 +2,8 @@ from contextlib import ExitStack
 
 import concourse.mybir as mybir
 
-K, T, R, N, B = 512, 1024, 512, 512, 512
-FLOPS = 2 * K * R * T * 2 + 2 * K * N * T + 2 * R * N * B
+K, L, T, R, N, B = 512, 512, 1024, 512, 512, 512
+FLOPS = 2 * (K + L) * R * T + 2 * R * N * B + 2 * K * N * T
 
 F32 = mybir.dt.float32
 BF16 = mybir.dt.bfloat16
@@ -15,6 +15,16 @@ ALU = mybir.AluOpType
 ACT = mybir.ActivationFunctionType
 
 P = 128
+PACK = 4
+QUADS = 4
+BANK = 512
+COLS = 512
+UNIT = 128
+CHUNK = 2 * UNIT
+CHUNKS = T // CHUNK
+HALF = T // 2
+Z_BANKS = 3
+WARM_PASSES = 4
 WA, WC, WY, WB = 0, 1, 2, 3
 XT, XQ = 0, 1
 
@@ -32,259 +42,261 @@ def tile_mix_hidden_peaks_of_pairs_pl_kernel(
         def sbuf(name, width, dtype):
             return sb.tile([P, width], dtype, name=name, align_bytes=256)
 
-        raw_sc = sbuf("raw_sc", 512, U8)
-        stage = sbuf("stage", 1024, U8)
-        plane = sbuf("plane", 4096, U8)
-        raw_w = [sbuf("raw_w%d" % w, 512, I32) for w in (WA, WC, WY)]
-        raw_wb = sbuf("raw_wb", 1024, U8)
-        dealt = [sbuf("dealt%d" % w, 512, I32) for w in (WA, WC, WY)]
-        dealt_wb = sbuf("dealt_wb", 1024, U8)
-        x = [sbuf("x%d" % s, 2048, U8) for s in (XT, XQ)]
-        odd_sb = [sbuf("odd%d" % u, 256, F32) for u in range(8)]
-        hid = [sbuf("hid%d" % c, 512, BF16) for c in range(4)]
-        hq = [sbuf("hq%d" % c, 128, I32) for c in range(4)]
-        hs = [sbuf("hs%d" % c, 128, U8) for c in range(4)]
-        th_sb = [sbuf("th%d" % c, 512, F32) for c in range(4)]
-        y = [sbuf("y%d" % c, 1024, F32) for c in range(4)]
-        yb = [sbuf("yb%d" % c, 1024, BF16) for c in range(4)]
-        yq = sbuf("yq", 1024, I32)
-        ys = sbuf("ys", 1024, U8)
-        zb = [ps.tile([P, 512], F32, name="zb%d" % i) for i in range(3)]
-        qb = [ps.tile([P, 512], F32, name="qb%d" % i) for i in range(4)]
-        pb = ps.tile([P, 512], F32, name="pb")
+        raw_scales = sbuf("raw_scales", 2 * COLS, U8)
+        staged = sbuf("staged", 2 * (COLS + HALF), U8)
+        planes = [sbuf("plane%d" % h, 2 * (COLS + HALF), U8) for h in range(2)]
+        raw_w = [sbuf("raw_w%d" % w, COLS, I32) for w in (WA, WC, WY)]
+        dealt_w = [sbuf("dealt_w%d" % w, COLS, I32) for w in (WA, WC, WY)]
+        raw_wb = sbuf("raw_wb", 2 * COLS, U8)
+        dealt_wb = sbuf("dealt_wb", 2 * COLS, U8)
+        x = [[sbuf("x%d_%d" % (s, h), 2 * HALF, U8) for h in range(2)] for s in (XT, XQ)]
+        odd_z = [sbuf("odd_z%d" % u, BANK // 2, F32) for u in range(2 * CHUNKS)]
+        hid = [sbuf("hid%d" % c, BANK, BF16) for c in range(CHUNKS)]
+        hid_words = [sbuf("hid_words%d" % c, P, I32) for c in range(CHUNKS)]
+        hid_scales = [sbuf("hid_scales%d" % c, P, U8) for c in range(CHUNKS)]
+        tanh_p = [sbuf("tanh_p%d" % c, BANK, F32) for c in range(CHUNKS)]
+        y = [sbuf("y%d" % c, PACK * CHUNK, F32) for c in range(CHUNKS)]
+        y_bf16 = [sbuf("y_bf16_%d" % c, PACK * CHUNK, BF16) for c in range(CHUNKS)]
+        y_words = sbuf("y_words", T, I32)
+        y_scales = sbuf("y_scales", T, U8)
+        zero = sbuf("zero", 1, F32)
+        tanh_zero = sbuf("tanh_zero", 1, F32)
+        z_banks = [ps.tile([P, BANK], F32, name="z_bank%d" % i) for i in range(Z_BANKS)]
+        q_banks = [ps.tile([P, BANK], F32, name="q_bank%d" % i) for i in range(4)]
+        p_bank = ps.tile([P, BANK], F32, name="p_bank")
 
-        def w_scale(w, j):
-            return plane[:, 1024 * w + 128 * j : 1024 * w + 128 * (j + 1)]
+        out_rows = out_0.rearrange("(m j) t -> m j t", j=PACK)
+        out_words = out_1[0].rearrange("m t j -> m (t j)").bitcast(I32)
 
-        def x_scale(s, t0, n):
-            c0 = 1024 * (2 * (t0 // 512) + s) + 512 + t0 % 512
-            return plane[:, c0 : c0 + n]
+        def load_weight_scales(queue, w, src):
+            h, side = divmod(w, 2)
+            dst = raw_scales[:, COLS * h : COLS * (h + 1)].bitcast(I32)
+            queue.dma_start(out=dst[side:32:2, :], in_=src[0].bitcast(I32))
 
-        def x_codes(s, t0, n):
-            return x[s][:, 2 * t0 : 2 * (t0 + n)].bitcast(FP4X4)
+        def load_token_scales(queue, s, src):
+            dst = staged[:].rearrange("m (h c) -> m h c", h=2)[:, :, COLS:].bitcast(I32)
+            queue.dma_start(out=dst[s:32:2], in_=src[0].rearrange("g (h c) -> g h c", h=2).bitcast(I32))
 
-        def load_w_scales(eng, w, src):
-            eng.dma_start(out=raw_sc[:].bitcast(I32)[w:64:4, :], in_=src[0].bitcast(I32))
+        def load_weight(queue, w, src):
+            queue.dma_start(out=raw_w[w][:], in_=src[0].rearrange("m n j -> m (n j)").bitcast(I32))
 
-        def load_x_scales(eng, s, src):
-            eng.dma_start(
-                out=stage[:].bitcast(I32)[s:64:2, 128:256],
-                in_=src[0].rearrange("q (h c) -> (q h) c", h=2).bitcast(I32),
+        def load_tokens(queue, s, h, src):
+            cols = slice(2 * HALF * h, 2 * HALF * (h + 1))
+            queue.dma_start(out=x[s][h][:].bitcast(I32), in_=src[0][:, cols].bitcast(I32))
+
+        def deal_scales(h):
+            c0 = (COLS + HALF) * h
+            nc.vector.tensor_copy(
+                out=staged[:, c0 : c0 + COLS].rearrange("p (j m) -> p j m", j=PACK),
+                in_=raw_scales[:, COLS * h : COLS * (h + 1)].rearrange("p (m j) -> p j m", j=PACK),
             )
 
-        def load_w(w, src):
-            nc.sync.dma_start(out=raw_w[w][:], in_=src[0].rearrange("p n t -> p (n t)").bitcast(I32))
+        def fill_plane(queue, h):
+            c0 = (COLS + HALF) * h
+            src = staged[:, c0 : c0 + COLS + HALF].bitcast(I32)
+            for quad in range(QUADS):
+                queue.dma_start(
+                    out=planes[h][:].bitcast(I32)[32 * quad : 32 * quad + 4, :],
+                    in_=src[8 * quad : 8 * quad + 8, :],
+                )
 
-        def deal(w):
+        def deal_weight(w):
             nc.vector.tensor_copy(
-                out=dealt[w][:].rearrange("p (j m) -> p m j", j=4),
-                in_=raw_w[w][:].rearrange("p (m j) -> p m j", j=4),
+                out=dealt_w[w][:].rearrange("p (j m) -> p m j", j=PACK),
+                in_=raw_w[w][:].rearrange("p (m j) -> p m j", j=PACK),
             )
 
         def deal_wb():
             nc.vector.tensor_copy(
-                out=dealt_wb[:].rearrange("p (j m e) -> p j m e", j=4, e=2),
-                in_=raw_wb[:].rearrange("p (m j e) -> p j m e", j=4, e=2),
+                out=dealt_wb[:].rearrange("p (j m e) -> p j m e", j=PACK, e=2),
+                in_=raw_wb[:].rearrange("p (m j e) -> p j m e", j=PACK, e=2),
             )
 
-        def z(u):
-            bank = zb[u % 3]
-            for j in range(4):
-                for w, s in ((WA, XT), (WC, XQ)):
-                    nc.tensor.matmul_mx(
-                        out=bank[:, 128 * j : 128 * (j + 1)],
-                        lhsT=dealt[w][:, 128 * j : 128 * (j + 1)].bitcast(FP8X4),
-                        lhsT_scale=w_scale(w, j),
-                        rhs=x_codes(s, 128 * u, 128),
-                        rhs_scale=x_scale(s, 128 * u, 128),
-                        start=(w == WA),
-                        stop=(w == WC),
-                    )
+        def weight_scales(w, j):
+            h, side = divmod(w, 2)
+            c0 = (COLS + HALF) * side + P * j
+            return planes[h][:, c0 : c0 + P]
 
-        def pairs(u):
-            return zb[u % 3][:].rearrange("p (j b e) -> p b j e", j=4, e=2)
+        def weight_times_tokens(out, w, j, s, t0, n, start, stop):
+            h, t_in_half = divmod(t0, HALF)
+            c0 = (COLS + HALF) * s + COLS + t_in_half
+            nc.tensor.matmul_mx(
+                out=out,
+                lhsT=dealt_w[w][:, P * j : P * (j + 1)].bitcast(FP8X4),
+                lhsT_scale=weight_scales(w, j),
+                rhs=x[s][h][:, 2 * t_in_half : 2 * (t_in_half + n)].bitcast(FP4X4),
+                rhs_scale=planes[h][:, c0 : c0 + n],
+                start=start,
+                stop=stop,
+            )
 
-        def hid_half(u):
-            return hid[u // 2][:, 256 * (u % 2) : 256 * (u % 2 + 1)].rearrange("p (b j) -> p b j", j=4)
+        def z_unit(u):
+            for j in range(PACK):
+                out = z_banks[u % Z_BANKS][:, UNIT * j : UNIT * (j + 1)]
+                weight_times_tokens(out, WA, j, XT, UNIT * u, UNIT, True, False)
+                weight_times_tokens(out, WC, j, XQ, UNIT * u, UNIT, False, True)
 
-        def red(u):
-            nc.vector.tensor_reduce(out=hid_half(u), in_=pairs(u), axis=mybir.AxisListType.X, op=ALU.max)
+        def z_pairs(u):
+            return z_banks[u % Z_BANKS][:].rearrange("p (j b e) -> p b j e", j=PACK, e=2)
 
-        def odd(u):
-            nc.scalar.copy(out=odd_sb[u][:].rearrange("p (b j) -> p b j", j=4), in_=pairs(u)[:, :, :, 1])
+        def by_pair(ap):
+            return ap.rearrange("p (b j) -> p b j", j=PACK)
 
-        def mx(u):
+        def hid_unit(u):
+            c, h = divmod(u, 2)
+            return by_pair(hid[c][:, BANK // 2 * h : BANK // 2 * (h + 1)])
+
+        def peak_alone(u):
+            nc.vector.tensor_reduce(out=hid_unit(u), in_=z_pairs(u), axis=mybir.AxisListType.X, op=ALU.max)
+
+        def copy_odd(u):
+            nc.scalar.copy(out=by_pair(odd_z[u][:]), in_=z_pairs(u)[:, :, :, 1])
+
+        def peak_shared(u):
             nc.vector.tensor_tensor(
-                out=hid_half(u), in0=pairs(u)[:, :, :, 0],
-                in1=odd_sb[u][:].rearrange("p (b j) -> p b j", j=4), op=ALU.max,
+                out=hid_unit(u), in0=z_pairs(u)[:, :, :, 0], in1=by_pair(odd_z[u][:]), op=ALU.max
             )
 
-        def qh(c):
-            nc.vector.quantize_mx(out=hq[c][:].bitcast(FP8X4), scales=hs[c][:], in_=hid[c][:])
+        def quantise_hid(c):
+            nc.vector.quantize_mx(out=hid_words[c][:].bitcast(FP8X4), scales=hid_scales[c][:], in_=hid[c][:])
 
-        def p(c):
-            for i in range(4):
+        def p_chunk(c):
+            for j in range(PACK):
                 nc.tensor.matmul_mx(
-                    out=pb[:, 128 * i : 128 * (i + 1)],
-                    lhsT=dealt_wb[:, 256 * i : 256 * (i + 1)].bitcast(FP4X4),
-                    lhsT_scale=w_scale(WB, i),
-                    rhs=hq[c][:].bitcast(FP8X4),
-                    rhs_scale=hs[c][:],
+                    out=p_bank[:, P * j : P * (j + 1)],
+                    lhsT=dealt_wb[:, 2 * P * j : 2 * P * (j + 1)].bitcast(FP4X4),
+                    lhsT_scale=weight_scales(WB, j),
+                    rhs=hid_words[c][:].bitcast(FP8X4),
+                    rhs_scale=hid_scales[c][:],
                     start=True,
                     stop=True,
                 )
 
-        def th(c):
-            nc.scalar.activation(out=th_sb[c][:], in_=pb[:], func=ACT.Tanh)
+        def tanh_chunk(c):
+            nc.scalar.activation(out=tanh_p[c][:], in_=p_bank[:], func=ACT.Tanh)
 
-        def q(c):
-            for i in range(4):
-                bank = qb[2 * (c % 2) + i // 2]
-                nc.tensor.matmul_mx(
-                    out=bank[:, 256 * (i % 2) : 256 * (i % 2 + 1)],
-                    lhsT=dealt[WY][:, 128 * i : 128 * (i + 1)].bitcast(FP8X4),
-                    lhsT_scale=w_scale(WY, i),
-                    rhs=x_codes(XT, 256 * c, 256),
-                    rhs_scale=x_scale(XT, 256 * c, 256),
-                    start=True,
-                    stop=True,
-                )
+        def q_bank(c, h):
+            return q_banks[2 * (c % 2) + h]
 
-        rows = out_0.rearrange("(p i) t -> p i t", i=4)
+        def q_chunk(c):
+            for j in range(PACK):
+                h, slot = divmod(j, 2)
+                out = q_bank(c, h)[:, CHUNK * slot : CHUNK * (slot + 1)]
+                weight_times_tokens(out, WY, j, XT, CHUNK * c, CHUNK, True, True)
 
-        def add(c, h):
-            part = y[c][:, 512 * h : 512 * (h + 1)]
+        def add_and_store(c, h):
+            part = y[c][:, BANK * h : BANK * (h + 1)]
+            twice = tanh_p[c][:, BANK // 2 * h : BANK // 2 * (h + 1)].unsqueeze(2).broadcast_to([P, BANK // 2, 2])
             nc.vector.tensor_tensor(
                 out=part.rearrange("p (b e) -> p b e", e=2),
-                in0=qb[2 * (c % 2) + h][:].rearrange("p (b e) -> p b e", e=2),
-                in1=th_sb[c][:, 256 * h : 256 * (h + 1)].unsqueeze(2).broadcast_to([P, 256, 2]),
+                in0=q_bank(c, h)[:].rearrange("p (b e) -> p b e", e=2),
+                in1=twice,
                 op=ALU.add,
             )
             nc.sync.dma_start(
-                out=rows[:, 2 * h : 2 * h + 2, 256 * c : 256 * (c + 1)],
-                in_=part.rearrange("p (i t) -> p i t", i=2),
+                out=out_rows[:, 2 * h : 2 * h + 2, CHUNK * c : CHUNK * (c + 1)],
+                in_=part.rearrange("p (j t) -> p j t", j=2),
             )
 
-        def cast_views(u):
+        def round_unit(copy, u):
             c, h = divmod(u, 2)
-            src = y[c][:].rearrange("p (i h g e) -> p h g i e", i=4, h=2, e=4)[:, h]
-            dst = yb[c][:, 512 * h : 512 * (h + 1)].rearrange("p (g e i) -> p g i e", e=4, i=4)
-            return dst, src
+            src = y[c][:].rearrange("p (j h g e) -> p h g j e", j=PACK, h=2, e=4)[:, h]
+            dst = y_bf16[c][:, BANK * h : BANK * (h + 1)].rearrange("p (g e j) -> p g j e", e=4, j=PACK)
+            copy(out=dst, in_=src)
 
-        def cS(u):
-            dst, src = cast_views(u)
-            nc.scalar.copy(out=dst, in_=src)
-
-        def cV(u):
-            dst, src = cast_views(u)
-            nc.vector.tensor_copy(out=dst, in_=src)
-
-        words = out_1[0].rearrange("p c r -> p (c r)").bitcast(I32)
-
-        def quant_y(c, t0, n):
-            cols = slice(256 * c + t0, 256 * c + t0 + n)
-            nc.vector.quantize_mx(out=yq[:, cols].bitcast(FP8X4), scales=ys[:, cols], in_=yb[c][:, 4 * t0 : 4 * (t0 + n)])
-
-        def st1(c):
-            nc.sync.dma_start(out=words[:, 256 * c : 256 * (c + 1)], in_=yq[:, 256 * c : 256 * (c + 1)])
-
-        def qY(c):
-            quant_y(c, 0, 256)
-            st1(c)
-
-        def qy(u):
-            quant_y(u // 2, 128 * (u % 2), 128)
-
-
-        nc.vector.memset(raw_sc[:].bitcast(I32)[64:128, :], 0)
-        nc.vector.memset(plane[:].bitcast(I32), 0)
-        load_w_scales(nc.sync, WA, wa_scales)
-        load_w_scales(nc.scalar, WY, wy_scales)
-        load_w_scales(nc.sync, WC, wc_scales)
-        load_w_scales(nc.scalar, WB, wb_scales)
-        load_x_scales(nc.sync, XT, xt_scales)
-        load_x_scales(nc.scalar, XQ, xq_scales)
-        load_w(WA, wa_words)
-        load_w(WC, wc_words)
-        nc.sync.dma_start(out=x[XT][:].bitcast(I32), in_=xt_words[0].bitcast(I32))
-        nc.sync.dma_start(out=x[XQ][:].bitcast(I32), in_=xq_words[0].bitcast(I32))
-        load_w(WY, wy_words)
-        nc.sync.dma_start(out=raw_wb[:].bitcast(I32), in_=wb_words[0].bitcast(I32))
-        nc.vector.tensor_copy(
-            out=stage[:, 0:512].rearrange("p (j m) -> p j m", j=4),
-            in_=raw_sc[:].rearrange("p (m j) -> p j m", j=4),
-        )
-        for quad in range(4):
-            nc.scalar.dma_start(
-                out=plane[:].bitcast(I32)[32 * quad : 32 * quad + 4, :],
-                in_=stage[:].bitcast(I32)[16 * quad : 16 * quad + 16, :],
+        def quantise_y(t0, n):
+            c, t_in_chunk = divmod(t0, CHUNK)
+            nc.vector.quantize_mx(
+                out=y_words[:, t0 : t0 + n].bitcast(FP8X4),
+                scales=y_scales[:, t0 : t0 + n],
+                in_=y_bf16[c][:, PACK * t_in_chunk : PACK * (t_in_chunk + n)],
             )
-        deal(WA)
-        deal(WC)
 
-        deal(WY)
+        def store_words(c):
+            cols = slice(CHUNK * c, CHUNK * (c + 1))
+            nc.sync.dma_start(out=out_words[:, cols], in_=y_words[:, cols])
+
+        nc.vector.memset(zero[:], 0.0)
+        nc.vector.memset(raw_scales[:].bitcast(I32)[32:64, :], 0)
+        nc.vector.memset(raw_scales[:].bitcast(I32)[64:128, :], 0)
+        for plane in planes:
+            nc.vector.memset(plane[:].bitcast(I32), 0)
+
+        load_weight_scales(nc.sync, WA, wa_scales)
+        load_weight_scales(nc.scalar, WC, wc_scales)
+        load_token_scales(nc.sync, XT, xt_scales)
+        load_token_scales(nc.scalar, XQ, xq_scales)
+        load_weight_scales(nc.sync, WY, wy_scales)
+        load_weight_scales(nc.scalar, WB, wb_scales)
+        nc.scalar.activation(out=tanh_zero[:], in_=zero[:], func=ACT.Tanh)
+        load_weight(nc.sync, WA, wa_words)
+        load_weight(nc.sync, WC, wc_words)
+        load_tokens(nc.sync, XT, 0, xt_words)
+        load_tokens(nc.sync, XQ, 0, xq_words)
+        deal_scales(0)
+        fill_plane(nc.scalar, 0)
+        nc.scalar.dma_start(out=raw_wb[:].bitcast(I32), in_=wb_words[0].bitcast(I32))
+        load_weight(nc.scalar, WY, wy_words)
+        deal_scales(1)
+        fill_plane(nc.scalar, 1)
+        load_tokens(nc.scalar, XT, 1, xt_words)
+        load_tokens(nc.scalar, XQ, 1, xq_words)
+
+        for warm_pass in range(WARM_PASSES):
+            nc.tensor.matmul_mx(
+                out=p_bank[:],
+                lhsT=raw_w[WA][:, 0:P].bitcast(FP8X4),
+                lhsT_scale=raw_scales[:, 0:P],
+                rhs=raw_w[WA][:, 0 : BANK // 2].bitcast(FP4X4),
+                rhs_scale=raw_scales[:, 0:BANK],
+                start=True,
+                stop=True,
+            )
+
+        deal_weight(WA)
+        deal_weight(WC)
         deal_wb()
-        z(0)
-        z(1)
-        red(0)
-        red(1)
-        z(2)
-        qh(0)
-        red(2)
-        z(3)
-        p(0)
-        th(0)
-        red(3)
-        q(0)
-        qh(1)
-        z(4)
-        odd(4)
-        add(0, 0)
-        z(5)
-        p(1)
-        mx(4)
-        odd(5)
-        add(0, 1)
-        th(1)
-        mx(5)
-        z(6)
-        q(1)
-        cS(0)
-        qh(2)
-        odd(6)
-        z(7)
-        p(2)
-        add(1, 0)
-        cS(1)
-        mx(6)
-        odd(7)
-        add(1, 1)
-        q(2)
-        mx(7)
-        th(2)
-        qY(0)
-        qh(3)
-        p(3)
-        q(3)
-        cS(2)
-        add(2, 0)
-        th(3)
-        add(2, 1)
-        cS(3)
-        add(3, 0)
-        cS(4)
-        qY(1)
-        add(3, 1)
-        cS(5)
-        cV(7)
-        cS(6)
-        qY(2)
-        qy(7)
-        qy(6)
-        st1(3)
-        for quad in range(4):
-            eng = nc.scalar if quad % 2 else nc.sync
-            eng.dma_start(
+
+        for u in (0, 1):
+            z_unit(u)
+            peak_alone(u)
+        deal_weight(WY)
+        quantise_hid(0)
+
+        last = CHUNKS - 1
+        for c in range(-1, CHUNKS):
+            hidden, second, sums, done = c + 2, c + 1, c, c - 1
+            for h in range(2):
+                if hidden <= last:
+                    z_unit(2 * hidden + h)
+                if sums >= 0:
+                    add_and_store(sums, h)
+                if hidden <= last:
+                    copy_odd(2 * hidden + h)
+            if second <= last:
+                p_chunk(second)
+                tanh_chunk(second)
+                q_chunk(second)
+            if hidden <= last:
+                peak_shared(2 * hidden)
+                peak_shared(2 * hidden + 1)
+            if done >= 0:
+                quantise_y(CHUNK * done, CHUNK)
+                store_words(done)
+            if hidden <= last:
+                quantise_hid(hidden)
+            if 0 <= sums < last:
+                round_unit(nc.scalar.copy, 2 * sums)
+                round_unit(nc.scalar.copy, 2 * sums + 1)
+
+        round_unit(nc.scalar.copy, 2 * last)
+        round_unit(nc.vector.tensor_copy, 2 * last + 1)
+        quantise_y(T - UNIT, UNIT)
+        quantise_y(T - CHUNK, UNIT)
+        store_words(last)
+        for quad in range(QUADS):
+            queue = nc.scalar if quad % 2 else nc.sync
+            queue.dma_start(
                 out=out_2[0, 4 * quad : 4 * quad + 4, :].bitcast(I32),
-                in_=ys[:].bitcast(I32)[32 * quad : 32 * quad + 4, :],
+                in_=y_scales[:].bitcast(I32)[32 * quad : 32 * quad + 4, :],
             )

@@ -91,19 +91,19 @@ def tile_mix_hidden_peaks_of_pairs_pl_kernel(
                 in_=raw_scales[:, COLS * h : COLS * (h + 1)].rearrange("p (m j) -> p j m", j=PACK),
             )
 
-        def fill_plane(queue, h):
+        def fill_plane(queues, h):
             c0 = (COLS + HALF) * h
             src = staged[:, c0 : c0 + COLS + HALF].bitcast(I32)
             for quad in range(QUADS):
-                queue.dma_start(
+                queues[quad % len(queues)].dma_start(
                     out=planes[h][:].bitcast(I32)[32 * quad : 32 * quad + 4, :],
                     in_=src[8 * quad : 8 * quad + 8, :],
                 )
 
         def deal_weight(w):
             nc.vector.tensor_copy(
-                out=dealt_w[w][:].rearrange("p (j m) -> p m j", j=PACK),
-                in_=raw_w[w][:].rearrange("p (m j) -> p m j", j=PACK),
+                out=dealt_w[w][:].rearrange("p (j a b) -> p a j b", j=PACK, b=4),
+                in_=raw_w[w][:].rearrange("p (a b j) -> p a j b", j=PACK, b=4),
             )
 
         def deal_wb():
@@ -173,7 +173,9 @@ def tile_mix_hidden_peaks_of_pairs_pl_kernel(
                 )
 
         def tanh_chunk(c):
-            nc.scalar.activation(out=tanh_p[c][:], in_=p_bank[:], func=ACT.Tanh)
+            for h in range(2):
+                cols = slice(BANK // 2 * h, BANK // 2 * (h + 1))
+                nc.scalar.activation(out=tanh_p[c][:, cols], in_=p_bank[:, cols], func=ACT.Tanh)
 
         def q_bank(c, h):
             return q_banks[2 * (c % 2) + h]
@@ -234,11 +236,11 @@ def tile_mix_hidden_peaks_of_pairs_pl_kernel(
         load_tokens(nc.sync, XT, 0, xt_words)
         load_tokens(nc.sync, XQ, 0, xq_words)
         deal_scales(0)
-        fill_plane(nc.scalar, 0)
+        fill_plane((nc.scalar, nc.sync), 0)
         nc.scalar.dma_start(out=raw_wb[:].bitcast(I32), in_=wb_words[0].bitcast(I32))
         load_weight(nc.scalar, WY, wy_words)
         deal_scales(1)
-        fill_plane(nc.scalar, 1)
+        fill_plane((nc.scalar,), 1)
         load_tokens(nc.scalar, XT, 1, xt_words)
         load_tokens(nc.scalar, XQ, 1, xq_words)
 
@@ -280,17 +282,22 @@ def tile_mix_hidden_peaks_of_pairs_pl_kernel(
             if hidden <= last:
                 peak_shared(2 * hidden)
                 peak_shared(2 * hidden + 1)
-            if done >= 0:
+            if sums == 0:
+                round_unit(nc.vector.tensor_copy, 0)
+            if 0 <= done < last - 1:
                 quantise_y(CHUNK * done, CHUNK)
                 store_words(done)
             if hidden <= last:
                 quantise_hid(hidden)
-            if 0 <= sums < last:
+            if 0 < sums < last:
                 round_unit(nc.scalar.copy, 2 * sums)
+            if 0 <= sums < last:
                 round_unit(nc.scalar.copy, 2 * sums + 1)
 
         round_unit(nc.scalar.copy, 2 * last)
         round_unit(nc.vector.tensor_copy, 2 * last + 1)
+        quantise_y(CHUNK * (last - 1), CHUNK)
+        store_words(last - 1)
         quantise_y(T - UNIT, UNIT)
         quantise_y(T - CHUNK, UNIT)
         store_words(last)

from contextlib import ExitStack

import concourse.mybir as mybir

K, L, T, R, N, B = 512, 512, 1024, 512, 512, 512
FLOPS = 2 * (K + L) * R * T + 2 * R * N * B + 2 * K * N * T

F32 = mybir.dt.float32
BF16 = mybir.dt.bfloat16
I32 = mybir.dt.int32
U8 = mybir.dt.uint8
FP8X4 = mybir.dt.float8_e4m3fn_x4
FP4X4 = mybir.dt.float4_e2m1fn_x4
ALU = mybir.AluOpType
ACT = mybir.ActivationFunctionType

P = 128
PACK = 4
QUADS = 4
BANK = 512
COLS = 512
UNIT = 128
CHUNK = 2 * UNIT
CHUNKS = T // CHUNK
HALF = T // 2
Z_BANKS = 3
WARM_PASSES = 4
WA, WC, WY, WB = 0, 1, 2, 3
XT, XQ = 0, 1


def tile_mix_hidden_peaks_of_pairs_pl_kernel(
    tc, xt_words, xt_scales, wa_words, wa_scales, xq_words, xq_scales, wc_words, wc_scales,
    wb_words, wb_scales, wy_words, wy_scales, out_0, out_1, out_2,
):
    nc = tc.nc
    with ExitStack() as ctx:
        sb = ctx.enter_context(tc.tile_pool(name="sb", bufs=1))
        ps = ctx.enter_context(tc.psum_pool(name="ps", bufs=1))
        ctx.enter_context(tc.manual_schedule())

        def sbuf(name, width, dtype):
            return sb.tile([P, width], dtype, name=name, align_bytes=256)

        raw_scales = sbuf("raw_scales", 2 * COLS, U8)
        staged = sbuf("staged", 2 * (COLS + HALF), U8)
        planes = [sbuf("plane%d" % h, 2 * (COLS + HALF), U8) for h in range(2)]
        raw_w = [sbuf("raw_w%d" % w, COLS, I32) for w in (WA, WC, WY)]
        dealt_w = [sbuf("dealt_w%d" % w, COLS, I32) for w in (WA, WC, WY)]
        raw_wb = sbuf("raw_wb", 2 * COLS, U8)
        dealt_wb = sbuf("dealt_wb", 2 * COLS, U8)
        x = [[sbuf("x%d_%d" % (s, h), 2 * HALF, U8) for h in range(2)] for s in (XT, XQ)]
        odd_z = [sbuf("odd_z%d" % u, BANK // 2, F32) for u in range(2 * CHUNKS)]
        hid = [sbuf("hid%d" % c, BANK, BF16) for c in range(CHUNKS)]
        hid_words = [sbuf("hid_words%d" % c, P, I32) for c in range(CHUNKS)]
        hid_scales = [sbuf("hid_scales%d" % c, P, U8) for c in range(CHUNKS)]
        tanh_p = [sbuf("tanh_p%d" % c, BANK, F32) for c in range(CHUNKS)]
        y = [sbuf("y%d" % c, PACK * CHUNK, F32) for c in range(CHUNKS)]
        y_bf16 = [sbuf("y_bf16_%d" % c, PACK * CHUNK, BF16) for c in range(CHUNKS)]
        y_words = sbuf("y_words", T, I32)
        y_scales = sbuf("y_scales", T, U8)
        zero = sbuf("zero", 1, F32)
        tanh_zero = sbuf("tanh_zero", 1, F32)
        z_banks = [ps.tile([P, BANK], F32, name="z_bank%d" % i) for i in range(Z_BANKS)]
        q_banks = [ps.tile([P, BANK], F32, name="q_bank%d" % i) for i in range(4)]
        p_bank = ps.tile([P, BANK], F32, name="p_bank")

        out_rows = out_0.rearrange("(m j) t -> m j t", j=PACK)
        out_words = out_1[0].rearrange("m t j -> m (t j)").bitcast(I32)

        def load_weight_scales(queue, w, src):
            h, side = divmod(w, 2)
            dst = raw_scales[:, COLS * h : COLS * (h + 1)].bitcast(I32)
            queue.dma_start(out=dst[side:32:2, :], in_=src[0].bitcast(I32))

        def load_token_scales(queue, s, src):
            dst = staged[:].rearrange("m (h c) -> m h c", h=2)[:, :, COLS:].bitcast(I32)
            queue.dma_start(out=dst[s:32:2], in_=src[0].rearrange("g (h c) -> g h c", h=2).bitcast(I32))

        def load_weight(queue, w, src):
            queue.dma_start(out=raw_w[w][:], in_=src[0].rearrange("m n j -> m (n j)").bitcast(I32))

        def load_tokens(queue, s, h, src):
            cols = slice(2 * HALF * h, 2 * HALF * (h + 1))
            queue.dma_start(out=x[s][h][:].bitcast(I32), in_=src[0][:, cols].bitcast(I32))

        def deal_scales(h):
            c0 = (COLS + HALF) * h
            nc.vector.tensor_copy(
                out=staged[:, c0 : c0 + COLS].rearrange("p (j m) -> p j m", j=PACK),
                in_=raw_scales[:, COLS * h : COLS * (h + 1)].rearrange("p (m j) -> p j m", j=PACK),
            )

        def fill_plane(queues, h):
            c0 = (COLS + HALF) * h
            src = staged[:, c0 : c0 + COLS + HALF].bitcast(I32)
            for quad in range(QUADS):
                queues[quad % len(queues)].dma_start(
                    out=planes[h][:].bitcast(I32)[32 * quad : 32 * quad + 4, :],
                    in_=src[8 * quad : 8 * quad + 8, :],
                )

        def deal_weight(w):
            nc.vector.tensor_copy(
                out=dealt_w[w][:].rearrange("p (j a b) -> p a j b", j=PACK, b=4),
                in_=raw_w[w][:].rearrange("p (a b j) -> p a j b", j=PACK, b=4),
            )

        def deal_wb():
            nc.vector.tensor_copy(
                out=dealt_wb[:].rearrange("p (j m e) -> p j m e", j=PACK, e=2),
                in_=raw_wb[:].rearrange("p (m j e) -> p j m e", j=PACK, e=2),
            )

        def weight_scales(w, j):
            h, side = divmod(w, 2)
            c0 = (COLS + HALF) * side + P * j
            return planes[h][:, c0 : c0 + P]

        def weight_times_tokens(out, w, j, s, t0, n, start, stop):
            h, t_in_half = divmod(t0, HALF)
            c0 = (COLS + HALF) * s + COLS + t_in_half
            nc.tensor.matmul_mx(
                out=out,
                lhsT=dealt_w[w][:, P * j : P * (j + 1)].bitcast(FP8X4),
                lhsT_scale=weight_scales(w, j),
                rhs=x[s][h][:, 2 * t_in_half : 2 * (t_in_half + n)].bitcast(FP4X4),
                rhs_scale=planes[h][:, c0 : c0 + n],
                start=start,
                stop=stop,
            )

        def z_unit(u):
            for j in range(PACK):
                out = z_banks[u % Z_BANKS][:, UNIT * j : UNIT * (j + 1)]
                weight_times_tokens(out, WA, j, XT, UNIT * u, UNIT, True, False)
                weight_times_tokens(out, WC, j, XQ, UNIT * u, UNIT, False, True)

        def z_pairs(u):
            return z_banks[u % Z_BANKS][:].rearrange("p (j b e) -> p b j e", j=PACK, e=2)

        def by_pair(ap):
            return ap.rearrange("p (b j) -> p b j", j=PACK)

        def hid_unit(u):
            c, h = divmod(u, 2)
            return by_pair(hid[c][:, BANK // 2 * h : BANK // 2 * (h + 1)])

        def peak_alone(u):
            nc.vector.tensor_reduce(out=hid_unit(u), in_=z_pairs(u), axis=mybir.AxisListType.X, op=ALU.max)

        def copy_odd(u):
            nc.scalar.copy(out=by_pair(odd_z[u][:]), in_=z_pairs(u)[:, :, :, 1])

        def peak_shared(u):
            nc.vector.tensor_tensor(
                out=hid_unit(u), in0=z_pairs(u)[:, :, :, 0], in1=by_pair(odd_z[u][:]), op=ALU.max
            )

        def quantise_hid(c):
            nc.vector.quantize_mx(out=hid_words[c][:].bitcast(FP8X4), scales=hid_scales[c][:], in_=hid[c][:])

        def p_chunk(c):
            for j in range(PACK):
                nc.tensor.matmul_mx(
                    out=p_bank[:, P * j : P * (j + 1)],
                    lhsT=dealt_wb[:, 2 * P * j : 2 * P * (j + 1)].bitcast(FP4X4),
                    lhsT_scale=weight_scales(WB, j),
                    rhs=hid_words[c][:].bitcast(FP8X4),
                    rhs_scale=hid_scales[c][:],
                    start=True,
                    stop=True,
                )

        def tanh_chunk(c):
            for h in range(2):
                cols = slice(BANK // 2 * h, BANK // 2 * (h + 1))
                nc.scalar.activation(out=tanh_p[c][:, cols], in_=p_bank[:, cols], func=ACT.Tanh)

        def q_bank(c, h):
            return q_banks[2 * (c % 2) + h]

        def q_chunk(c):
            for j in range(PACK):
                h, slot = divmod(j, 2)
                out = q_bank(c, h)[:, CHUNK * slot : CHUNK * (slot + 1)]
                weight_times_tokens(out, WY, j, XT, CHUNK * c, CHUNK, True, True)

        def add_and_store(c, h):
            part = y[c][:, BANK * h : BANK * (h + 1)]
            twice = tanh_p[c][:, BANK // 2 * h : BANK // 2 * (h + 1)].unsqueeze(2).broadcast_to([P, BANK // 2, 2])
            nc.vector.tensor_tensor(
                out=part.rearrange("p (b e) -> p b e", e=2),
                in0=q_bank(c, h)[:].rearrange("p (b e) -> p b e", e=2),
                in1=twice,
                op=ALU.add,
            )
            nc.sync.dma_start(
                out=out_rows[:, 2 * h : 2 * h + 2, CHUNK * c : CHUNK * (c + 1)],
                in_=part.rearrange("p (j t) -> p j t", j=2),
            )

        def round_unit(copy, u):
            c, h = divmod(u, 2)
            src = y[c][:].rearrange("p (j h g e) -> p h g j e", j=PACK, h=2, e=4)[:, h]
            dst = y_bf16[c][:, BANK * h : BANK * (h + 1)].rearrange("p (g e j) -> p g j e", e=4, j=PACK)
            copy(out=dst, in_=src)

        def quantise_y(t0, n):
            c, t_in_chunk = divmod(t0, CHUNK)
            nc.vector.quantize_mx(
                out=y_words[:, t0 : t0 + n].bitcast(FP8X4),
                scales=y_scales[:, t0 : t0 + n],
                in_=y_bf16[c][:, PACK * t_in_chunk : PACK * (t_in_chunk + n)],
            )

        def store_words(c):
            cols = slice(CHUNK * c, CHUNK * (c + 1))
            nc.sync.dma_start(out=out_words[:, cols], in_=y_words[:, cols])

        nc.vector.memset(zero[:], 0.0)
        nc.vector.memset(raw_scales[:].bitcast(I32)[32:64, :], 0)
        nc.vector.memset(raw_scales[:].bitcast(I32)[64:128, :], 0)
        for plane in planes:
            nc.vector.memset(plane[:].bitcast(I32), 0)

        load_weight_scales(nc.sync, WA, wa_scales)
        load_weight_scales(nc.scalar, WC, wc_scales)
        load_token_scales(nc.sync, XT, xt_scales)
        load_token_scales(nc.scalar, XQ, xq_scales)
        load_weight_scales(nc.sync, WY, wy_scales)
        load_weight_scales(nc.scalar, WB, wb_scales)
        nc.scalar.activation(out=tanh_zero[:], in_=zero[:], func=ACT.Tanh)
        load_weight(nc.sync, WA, wa_words)
        load_weight(nc.sync, WC, wc_words)
        load_tokens(nc.sync, XT, 0, xt_words)
        load_tokens(nc.sync, XQ, 0, xq_words)
        deal_scales(0)
        fill_plane((nc.scalar, nc.sync), 0)
        nc.scalar.dma_start(out=raw_wb[:].bitcast(I32), in_=wb_words[0].bitcast(I32))
        load_weight(nc.scalar, WY, wy_words)
        deal_scales(1)
        fill_plane((nc.scalar,), 1)
        load_tokens(nc.scalar, XT, 1, xt_words)
        load_tokens(nc.scalar, XQ, 1, xq_words)

        for warm_pass in range(WARM_PASSES):
            nc.tensor.matmul_mx(
                out=p_bank[:],
                lhsT=raw_w[WA][:, 0:P].bitcast(FP8X4),
                lhsT_scale=raw_scales[:, 0:P],
                rhs=raw_w[WA][:, 0 : BANK // 2].bitcast(FP4X4),
                rhs_scale=raw_scales[:, 0:BANK],
                start=True,
                stop=True,
            )

        deal_weight(WA)
        deal_weight(WC)
        deal_wb()

        for u in (0, 1):
            z_unit(u)
            peak_alone(u)
        deal_weight(WY)
        quantise_hid(0)

        last = CHUNKS - 1
        for c in range(-1, CHUNKS):
            hidden, second, sums, done = c + 2, c + 1, c, c - 1
            for h in range(2):
                if hidden <= last:
                    z_unit(2 * hidden + h)
                if sums >= 0:
                    add_and_store(sums, h)
                if hidden <= last:
                    copy_odd(2 * hidden + h)
            if second <= last:
                p_chunk(second)
                tanh_chunk(second)
                q_chunk(second)
            if hidden <= last:
                peak_shared(2 * hidden)
                peak_shared(2 * hidden + 1)
            if sums == 0:
                round_unit(nc.vector.tensor_copy, 0)
            if 0 <= done < last - 1:
                quantise_y(CHUNK * done, CHUNK)
                store_words(done)
            if hidden <= last:
                quantise_hid(hidden)
            if 0 < sums < last:
                round_unit(nc.scalar.copy, 2 * sums)
            if 0 <= sums < last:
                round_unit(nc.scalar.copy, 2 * sums + 1)

        round_unit(nc.scalar.copy, 2 * last)
        round_unit(nc.vector.tensor_copy, 2 * last + 1)
        quantise_y(CHUNK * (last - 1), CHUNK)
        store_words(last - 1)
        quantise_y(T - UNIT, UNIT)
        quantise_y(T - CHUNK, UNIT)
        store_words(last)
        for quad in range(QUADS):
            queue = nc.scalar if quad % 2 else nc.sync
            queue.dma_start(
                out=out_2[0, 4 * quad : 4 * quad + 4, :].bitcast(I32),
                in_=y_scales[:].bitcast(I32)[32 * quad : 32 * quad + 4, :],
            )
